import numpy as np
import ml_dtypes


def mxq(x, axis, fmt="e4m3"):
    dtype, down = {"e4m3": (ml_dtypes.float8_e4m3fn, 7), "e5m2": (ml_dtypes.float8_e5m2, 14)}[fmt]
    v = np.moveaxis(np.asarray(x, np.float32).astype(ml_dtypes.bfloat16).astype(np.float64), axis, -1)
    blocks = v.reshape(v.shape[:-1] + (-1, 32))
    amax = np.abs(blocks).max(-1, keepdims=True)
    byte = np.maximum(np.where(amax > 0, np.frexp(amax)[1] - 1 + 127, 0) - down, 1)
    scale = np.exp2(byte - 127.0)
    codes = (blocks / scale).astype(np.float32).astype(dtype).astype(np.float64)
    return np.moveaxis((codes * scale).reshape(v.shape), -1, axis)


WIDE = False


def mx_kscale(k):
    if not WIDE:
        return np.ones(k)
    levels = np.array([10, -10, 5, -5, 0])
    if k % 512:
        return np.exp2(np.random.permutation(np.resize(levels, k // 32))).repeat(32)
    a = np.empty((k // 512, 16))
    for p in range(k // 512):
        a[p, :8] = np.random.permutation(np.resize(levels, 8))
        for g in range(8):
            far = levels[np.abs(levels - a[p, g]) >= 10]
            a[p, g + 8] = far[np.random.randint(len(far))]
    return np.exp2(a.ravel()).repeat(32)


def f64(x):
    return np.asarray(x).astype(np.float64)


def striped(idx):
    return np.tile(np.asarray(idx).reshape(-1, 16).T, (8, 1)).astype(np.uint16)


def unstriped(offs):
    return offs[:16].T.reshape(-1).astype(np.int64)


B, N, T, D, DV, NQ = 1, 512, 1024, 512, 0, 128


def setup_inputs():
    n = np.random.standard_normal
    idx = np.random.permutation(T)[:B * N]
    s = mx_kscale(D)[:, None]
    return {
        "qT": (n((B, D, NQ)) * s * (1.00 / np.sqrt(D))).astype(np.float32),
        "kT": (n((D, T)) / s).astype(np.float32),
        "offs": striped(idx),
    }


def reference(qT, kT, offs):
    idx = unstriped(offs)
    pick = lambda x: x[:, idx].reshape(x.shape[0], B, N).transpose(1, 0, 2)
    a = mxq(f64(qT), 1, "e4m3").transpose(0, 2, 1) @ mxq(pick(f64(kT)), 1, "e4m3")
    out = np.zeros((B, NQ, T))
    for b in range(B):
        out[b][:, idx[b * N:(b + 1) * N]] = a[b]
    return out

@@ -1,0 +1,134 @@
+from contextlib import ExitStack
+
+import concourse.mybir as mybir
+
+SLOTS, TOKENS, FEATURES, QUERIES = 512, 1024, 512, 128
+P = 128
+PACK = 4
+CHUNK = 128
+OFFSETS_A_COLUMN = 16
+
+EARLY_SPLIT = 256
+LATE_SPLIT = 128
+LAST_CUT = 384
+SCATTER_SPLIT = 128
+
+FLOPS = 2 * QUERIES * FEATURES * SLOTS
+
+F32 = mybir.dt.float32
+BF16 = mybir.dt.bfloat16
+U32 = mybir.dt.uint32
+U16 = mybir.dt.uint16
+U8 = mybir.dt.uint8
+FP8X4 = mybir.dt.float8_e4m3fn_x4
+COPY = mybir.ActivationFunctionType.Copy
+
+
+def tile_attend_sddmm_kernel(tc, qT, kT, offs, out):
+    nc = tc.nc
+    k_rows = kT.rearrange("(p j) t -> j p t", j=PACK)
+    q_rows = qT[0].rearrange("(p j) q -> p j q", j=PACK)
+
+    with ExitStack() as ctx:
+        keep = ctx.enter_context(tc.tile_pool(name="keep", bufs=1))
+        psum = ctx.enter_context(tc.psum_pool(name="psum", bufs=1))
+
+        offsets = keep.tile([P, SLOTS // OFFSETS_A_COLUMN], U16, name="offsets")
+        planes = [keep.tile([P, TOKENS], F32, name=f"plane{j}") for j in range(PACK)]
+        q_raw = keep.tile([P, PACK, QUERIES], F32, name="q_raw")
+
+        whole = slice(0, TOKENS)
+        first_half = slice(0, TOKENS // 2)
+        second_half = slice(TOKENS // 2, TOKENS)
+        nc.sync.dma_start(planes[0][:, first_half], k_rows[0][:, first_half])
+        nc.sync.dma_start(planes[0][:, second_half], k_rows[0][:, second_half])
+        nc.sync.dma_start(offsets[:], offs)
+        for j in range(1, PACK):
+            nc.sync.dma_start(planes[j][:], k_rows[j])
+        nc.sync.dma_start(q_raw[:], q_rows)
+
+        window = keep.tile([P, TOKENS], F32, name="window")
+        nc.vector.memset(window[:], 0.0)
+
+        warm_in = keep.tile([P, 8], F32, name="warm_in")
+        warm_out = keep.tile([P, 8], F32, name="warm_out")
+        nc.vector.memset(warm_in[:], 0.0)
+        nc.scalar.activation(warm_out[:], warm_in[:], COPY)
+
+        rounded = [keep.tile([P, TOKENS], BF16, name=f"rounded{j}") for j in range(PACK)]
+        keys = keep.tile([P, SLOTS, PACK], BF16, align_bytes=64, name="keys")
+        q_grouped = keep.tile([P, QUERIES, PACK], BF16, align_bytes=64, tag="stage", name="q_grouped")
+        q_codes = keep.tile([P, QUERIES], U32, align_bytes=64, name="q_codes")
+        q_scales = keep.tile([P, QUERIES], U8, align_bytes=64, name="q_scales")
+
+        def listed(tile, lo, hi):
+            return tile[:].indirect(offsets[:, lo // OFFSETS_A_COLUMN : hi // OFFSETS_A_COLUMN])
+
+        def gather_on_vector(j, lo, hi):
+            nc.vector.tensor_copy(keys[:, lo:hi, j], listed(planes[j], lo, hi))
+
+        def gather_on_scalar(j, lo, hi):
+            nc.scalar.activation(keys[:, lo:hi, j], listed(rounded[j], lo, hi), COPY)
+
+        def cast_on_vector(j, columns):
+            nc.vector.tensor_copy(rounded[j][:, columns], planes[j][:, columns])
+
+        def cast_on_scalar(j, columns):
+            nc.scalar.activation(rounded[j][:, columns], planes[j][:, columns], COPY)
+
+        cast_on_vector(0, first_half)
+        cast_on_vector(0, second_half)
+        gather_on_scalar(0, 0, EARLY_SPLIT)
+        gather_on_vector(0, EARLY_SPLIT, SLOTS)
+        cast_on_vector(1, first_half)
+        cast_on_scalar(1, second_half)
+        gather_on_scalar(1, 0, EARLY_SPLIT)
+        gather_on_vector(1, EARLY_SPLIT, SLOTS)
+        cast_on_vector(2, whole)
+        gather_on_scalar(2, LATE_SPLIT, SLOTS)
+        gather_on_vector(2, 0, LATE_SPLIT)
+        cast_on_vector(3, whole)
+        gather_on_scalar(3, LATE_SPLIT, LAST_CUT)
+        gather_on_scalar(3, LAST_CUT, SLOTS)
+
+        result = keep.tile([QUERIES, SLOTS], F32, name="result")
+        first_codes = keep.tile([P, CHUNK], U32, align_bytes=64, name="first_codes")
+        scales = [keep.tile([P, CHUNK], U8, align_bytes=64, name=f"scales{c}") for c in range(SLOTS // CHUNK)]
+
+        gather_on_vector(3, 0, LATE_SPLIT)
+        nc.vector.tensor_copy(q_grouped[:], q_raw[:].rearrange("p j q -> p q j"))
+        nc.vector.quantize_mx(
+            out=q_codes[:].bitcast(FP8X4),
+            scales=q_scales[:],
+            in_=q_grouped[:].rearrange("p q j -> p (q j)"),
+        )
+
+        late_codes = keep.tile([P, SLOTS - CHUNK], U32, align_bytes=64, tag="stage", name="late_codes")
+
+        def codes_of(c):
+            if c == 0:
+                return first_codes[:]
+            return late_codes[:, (c - 1) * CHUNK : c * CHUNK]
+
+        for c in range(SLOTS // CHUNK):
+            slots = slice(c * CHUNK, (c + 1) * CHUNK)
+            nc.vector.quantize_mx(
+                out=codes_of(c).bitcast(FP8X4),
+                scales=scales[c][:],
+                in_=keys[:, slots, :].rearrange("p n j -> p (n j)"),
+            )
+            acc = psum.tile([QUERIES, CHUNK], F32, name=f"acc{c}")
+            nc.tensor.matmul_mx(
+                out=acc[:],
+                lhsT=q_codes[:].bitcast(FP8X4),
+                lhsT_scale=q_scales[:],
+                rhs=codes_of(c).bitcast(FP8X4),
+                rhs_scale=scales[c][:],
+                start=True,
+                stop=True,
+            )
+            nc.scalar.copy(result[:, slots], acc[:])
+
+        for lo, hi in ((0, SCATTER_SPLIT), (SCATTER_SPLIT, SLOTS)):
+            nc.vector.tensor_copy(listed(window, lo, hi), result[:, lo:hi])
+        nc.sync.dma_start(out[0], window[:])

@@ -7,12 +7,6 @@ P = 128
 PACK = 4
 CHUNK = 128
 OFFSETS_A_COLUMN = 16
-
-EARLY_SPLIT = 256
-LATE_SPLIT = 128
-LAST_CUT = 384
-SCATTER_SPLIT = 128
-
 FLOPS = 2 * QUERIES * FEATURES * SLOTS
 
 F32 = mybir.dt.float32
@@ -36,30 +30,13 @@ def tile_attend_sddmm_kernel(tc, qT, kT, offs, out):
         offsets = keep.tile([P, SLOTS // OFFSETS_A_COLUMN], U16, name="offsets")
         planes = [keep.tile([P, TOKENS], F32, name=f"plane{j}") for j in range(PACK)]
         q_raw = keep.tile([P, PACK, QUERIES], F32, name="q_raw")
-
-        whole = slice(0, TOKENS)
-        first_half = slice(0, TOKENS // 2)
-        second_half = slice(TOKENS // 2, TOKENS)
-        nc.sync.dma_start(planes[0][:, first_half], k_rows[0][:, first_half])
-        nc.sync.dma_start(planes[0][:, second_half], k_rows[0][:, second_half])
-        nc.sync.dma_start(offsets[:], offs)
-        for j in range(1, PACK):
-            nc.sync.dma_start(planes[j][:], k_rows[j])
-        nc.sync.dma_start(q_raw[:], q_rows)
-
         window = keep.tile([P, TOKENS], F32, name="window")
-        nc.vector.memset(window[:], 0.0)
-
-        warm_in = keep.tile([P, 8], F32, name="warm_in")
-        warm_out = keep.tile([P, 8], F32, name="warm_out")
-        nc.vector.memset(warm_in[:], 0.0)
-        nc.scalar.activation(warm_out[:], warm_in[:], COPY)
-
         rounded = [keep.tile([P, TOKENS], BF16, name=f"rounded{j}") for j in range(PACK)]
         keys = keep.tile([P, SLOTS, PACK], BF16, align_bytes=64, name="keys")
         q_grouped = keep.tile([P, QUERIES, PACK], BF16, align_bytes=64, tag="stage", name="q_grouped")
         q_codes = keep.tile([P, QUERIES], U32, align_bytes=64, name="q_codes")
         q_scales = keep.tile([P, QUERIES], U8, align_bytes=64, name="q_scales")
+        result = keep.tile([QUERIES, SLOTS], F32, name="result")
 
         def listed(tile, lo, hi):
             return tile[:].indirect(offsets[:, lo // OFFSETS_A_COLUMN : hi // OFFSETS_A_COLUMN])
@@ -70,65 +47,80 @@ def tile_attend_sddmm_kernel(tc, qT, kT, offs, out):
         def gather_on_scalar(j, lo, hi):
             nc.scalar.activation(keys[:, lo:hi, j], listed(rounded[j], lo, hi), COPY)
 
-        def cast_on_vector(j, columns):
-            nc.vector.tensor_copy(rounded[j][:, columns], planes[j][:, columns])
+        def cast_on_vector(j, lo, hi):
+            nc.vector.tensor_copy(rounded[j][:, lo:hi], planes[j][:, lo:hi])
 
-        def cast_on_scalar(j, columns):
-            nc.scalar.activation(rounded[j][:, columns], planes[j][:, columns], COPY)
+        def cast_on_scalar(j, lo, hi):
+            nc.scalar.activation(rounded[j][:, lo:hi], planes[j][:, lo:hi], COPY)
 
-        cast_on_vector(0, first_half)
-        cast_on_vector(0, second_half)
-        gather_on_scalar(0, 0, EARLY_SPLIT)
-        gather_on_vector(0, EARLY_SPLIT, SLOTS)
-        cast_on_vector(1, first_half)
-        cast_on_scalar(1, second_half)
-        gather_on_scalar(1, 0, EARLY_SPLIT)
-        gather_on_vector(1, EARLY_SPLIT, SLOTS)
-        cast_on_vector(2, whole)
-        gather_on_scalar(2, LATE_SPLIT, SLOTS)
-        gather_on_vector(2, 0, LATE_SPLIT)
-        cast_on_vector(3, whole)
-        gather_on_scalar(3, LATE_SPLIT, LAST_CUT)
-        gather_on_scalar(3, LAST_CUT, SLOTS)
-
-        result = keep.tile([QUERIES, SLOTS], F32, name="result")
-        first_codes = keep.tile([P, CHUNK], U32, align_bytes=64, name="first_codes")
-        scales = [keep.tile([P, CHUNK], U8, align_bytes=64, name=f"scales{c}") for c in range(SLOTS // CHUNK)]
-
-        gather_on_vector(3, 0, LATE_SPLIT)
-        nc.vector.tensor_copy(q_grouped[:], q_raw[:].rearrange("p j q -> p q j"))
-        nc.vector.quantize_mx(
-            out=q_codes[:].bitcast(FP8X4),
-            scales=q_scales[:],
-            in_=q_grouped[:].rearrange("p q j -> p (q j)"),
-        )
-
-        late_codes = keep.tile([P, SLOTS - CHUNK], U32, align_bytes=64, tag="stage", name="late_codes")
-
-        def codes_of(c):
-            if c == 0:
-                return first_codes[:]
-            return late_codes[:, (c - 1) * CHUNK : c * CHUNK]
-
-        for c in range(SLOTS // CHUNK):
-            slots = slice(c * CHUNK, (c + 1) * CHUNK)
+        def quantise_queries():
             nc.vector.quantize_mx(
-                out=codes_of(c).bitcast(FP8X4),
-                scales=scales[c][:],
-                in_=keys[:, slots, :].rearrange("p n j -> p (n j)"),
+                out=q_codes[:].bitcast(FP8X4),
+                scales=q_scales[:],
+                in_=q_grouped[:].rearrange("p q j -> p (q j)"),
             )
-            acc = psum.tile([QUERIES, CHUNK], F32, name=f"acc{c}")
+
+        def new_codes(width, name):
+            return keep.tile([P, width], U32, align_bytes=64, name=name)
+
+        def quantise(lo, hi, codes):
+            scales = keep.tile([P, hi - lo], U8, align_bytes=64, name=f"scales{lo}")
+            nc.vector.quantize_mx(
+                out=codes.bitcast(FP8X4),
+                scales=scales[:],
+                in_=keys[:, lo:hi, :].rearrange("p n j -> p (n j)"),
+            )
+            acc = psum.tile([QUERIES, hi - lo], F32, name=f"acc{lo}")
             nc.tensor.matmul_mx(
                 out=acc[:],
                 lhsT=q_codes[:].bitcast(FP8X4),
                 lhsT_scale=q_scales[:],
-                rhs=codes_of(c).bitcast(FP8X4),
-                rhs_scale=scales[c][:],
+                rhs=codes.bitcast(FP8X4),
+                rhs_scale=scales[:],
                 start=True,
                 stop=True,
             )
-            nc.scalar.copy(result[:, slots], acc[:])
+            return acc
 
-        for lo, hi in ((0, SCATTER_SPLIT), (SCATTER_SPLIT, SLOTS)):
+        def scatter(lo, hi):
             nc.vector.tensor_copy(listed(window, lo, hi), result[:, lo:hi])
+
+        def load(j):
+            nc.sync.dma_start(planes[j][:], k_rows[j])
+
+        load(0)
+        nc.sync.dma_start(offsets[:], offs)
+        load(1)
+        load(2)
+        load(3)
+        nc.sync.dma_start(q_raw[:], q_rows)
+        nc.vector.memset(window[:], 0.0)
+        cast_on_scalar(0, 768, 1024)
+        cast_on_vector(0, 0, 768)
+        gather_on_vector(0, 0, 160)
+        gather_on_scalar(0, 160, SLOTS)
+        cast_on_vector(1, 0, 1024)
+        gather_on_vector(1, 0, 160)
+        gather_on_scalar(1, 160, SLOTS)
+        cast_on_vector(2, 0, 1024)
+        gather_on_vector(2, 0, 128)
+        gather_on_scalar(2, 128, SLOTS)
+        cast_on_vector(3, 0, 1024)
+        gather_on_vector(3, 0, 128)
+        gather_on_scalar(3, 128, 384)
+        gather_on_scalar(3, 384, 512)
+        nc.gpsimd.tensor_scalar(q_grouped[:, 0:64, :], q_raw[:, :, 0:64].rearrange("p j q -> p q j"), 1.0, 0.0, mybir.AluOpType.mult, mybir.AluOpType.add)
+        nc.vector.tensor_copy(q_grouped[:, 64:128, :], q_raw[:, :, 64:128].rearrange("p j q -> p q j"))
+        quantise_queries()
+        acc = quantise(0, 128, new_codes(128, "codes0")[:])
+        nc.scalar.copy(result[:, 0:128], acc[:])
+        late = keep.tile([P, 384], U32, align_bytes=64, tag="stage", name="late")
+        acc = quantise(128, 256, late[:, 0:128])
+        nc.scalar.copy(result[:, 128:256], acc[:])
+        acc = quantise(256, 384, late[:, 128:256])
+        nc.scalar.copy(result[:, 256:384], acc[:])
+        acc = quantise(384, 512, late[:, 256:384])
+        nc.scalar.copy(result[:, 384:512], acc[:])
+        scatter(0, 128)
+        scatter(128, 512)
         nc.sync.dma_start(out[0], window[:])

@@ -109,8 +109,7 @@ def tile_attend_sddmm_kernel(tc, qT, kT, offs, out):
         gather_on_vector(3, 0, 128)
         gather_on_scalar(3, 128, 384)
         gather_on_scalar(3, 384, 512)
-        nc.gpsimd.tensor_scalar(q_grouped[:, 0:64, :], q_raw[:, :, 0:64].rearrange("p j q -> p q j"), 1.0, 0.0, mybir.AluOpType.mult, mybir.AluOpType.add)
-        nc.vector.tensor_copy(q_grouped[:, 64:128, :], q_raw[:, :, 64:128].rearrange("p j q -> p q j"))
+        nc.vector.tensor_copy(q_grouped[:, 0:128, :], q_raw[:, :, 0:128].rearrange("p j q -> p q j"))
         quantise_queries()
         acc = quantise(0, 128, new_codes(128, "codes0")[:])
         nc.scalar.copy(result[:, 0:128], acc[:])

@@ -7,6 +7,13 @@ P = 128
 PACK = 4
 CHUNK = 128
 OFFSETS_A_COLUMN = 16
+PLANE_ORDER = (0, 2, 3, 1)
+HALF = TOKENS // 2
+
+VECTOR_SLOTS = (192, CHUNK, 160, 160)
+VECTOR_CASTS = ((HALF, TOKENS), (0, TOKENS), (0, TOKENS), (0, TOKENS))
+LAST_CUT = 384
+
 FLOPS = 2 * QUERIES * FEATURES * SLOTS
 
 F32 = mybir.dt.float32
@@ -30,47 +37,61 @@ def tile_attend_sddmm_kernel(tc, qT, kT, offs, out):
         offsets = keep.tile([P, SLOTS // OFFSETS_A_COLUMN], U16, name="offsets")
         planes = [keep.tile([P, TOKENS], F32, name=f"plane{j}") for j in range(PACK)]
         q_raw = keep.tile([P, PACK, QUERIES], F32, name="q_raw")
+
+        nc.sync.dma_start(planes[0][:, :HALF], k_rows[0][:, :HALF])
+        nc.sync.dma_start(planes[0][:, HALF:], k_rows[0][:, HALF:])
+        nc.sync.dma_start(offsets[:], offs)
+        for j in PLANE_ORDER[1:]:
+            nc.sync.dma_start(planes[j][:], k_rows[j])
+        nc.sync.dma_start(q_raw[:], q_rows)
+
         window = keep.tile([P, TOKENS], F32, name="window")
+        nc.vector.memset(window[:], 0.0)
+
         rounded = [keep.tile([P, TOKENS], BF16, name=f"rounded{j}") for j in range(PACK)]
         keys = keep.tile([P, SLOTS, PACK], BF16, align_bytes=64, name="keys")
         q_grouped = keep.tile([P, QUERIES, PACK], BF16, align_bytes=64, tag="stage", name="q_grouped")
         q_codes = keep.tile([P, QUERIES], U32, align_bytes=64, name="q_codes")
         q_scales = keep.tile([P, QUERIES], U8, align_bytes=64, name="q_scales")
-        result = keep.tile([QUERIES, SLOTS], F32, name="result")
 
         def listed(tile, lo, hi):
             return tile[:].indirect(offsets[:, lo // OFFSETS_A_COLUMN : hi // OFFSETS_A_COLUMN])
 
-        def gather_on_vector(j, lo, hi):
-            nc.vector.tensor_copy(keys[:, lo:hi, j], listed(planes[j], lo, hi))
-
-        def gather_on_scalar(j, lo, hi):
-            nc.scalar.activation(keys[:, lo:hi, j], listed(rounded[j], lo, hi), COPY)
-
-        def cast_on_vector(j, lo, hi):
+        for j in PLANE_ORDER:
+            lo, hi = VECTOR_CASTS[j]
+            if lo > 0:
+                nc.scalar.activation(rounded[j][:, :lo], planes[j][:, :lo], COPY)
             nc.vector.tensor_copy(rounded[j][:, lo:hi], planes[j][:, lo:hi])
+            if hi < TOKENS:
+                nc.scalar.activation(rounded[j][:, hi:], planes[j][:, hi:], COPY)
 
-        def cast_on_scalar(j, lo, hi):
-            nc.scalar.activation(rounded[j][:, lo:hi], planes[j][:, lo:hi], COPY)
+            bound = VECTOR_SLOTS[j]
+            nc.vector.tensor_copy(keys[:, :bound, j], listed(planes[j], 0, bound))
+            last_plane = j == PLANE_ORDER[-1]
+            for first, end in ((bound, LAST_CUT), (LAST_CUT, SLOTS)) if last_plane else ((bound, SLOTS),):
+                nc.scalar.activation(keys[:, first:end, j], listed(rounded[j], first, end), COPY)
 
-        def quantise_queries():
-            nc.vector.quantize_mx(
-                out=q_codes[:].bitcast(FP8X4),
-                scales=q_scales[:],
-                in_=q_grouped[:].rearrange("p q j -> p (q j)"),
-            )
+        nc.vector.tensor_copy(q_grouped[:], q_raw[:].rearrange("p j q -> p q j"))
+        nc.vector.quantize_mx(
+            out=q_codes[:].bitcast(FP8X4),
+            scales=q_scales[:],
+            in_=q_grouped[:].rearrange("p q j -> p (q j)"),
+        )
 
-        def new_codes(width, name):
-            return keep.tile([P, width], U32, align_bytes=64, name=name)
+        first_codes = keep.tile([P, CHUNK], U32, align_bytes=64, name="first_codes")
+        late_codes = keep.tile([P, SLOTS - CHUNK], U32, align_bytes=64, tag="stage", name="late_codes")
+        result = keep.tile([QUERIES, SLOTS], F32, name="result")
 
-        def quantise(lo, hi, codes):
-            scales = keep.tile([P, hi - lo], U8, align_bytes=64, name=f"scales{lo}")
+        for c in range(SLOTS // CHUNK):
+            slots = slice(c * CHUNK, (c + 1) * CHUNK)
+            codes = first_codes[:] if c == 0 else late_codes[:, (c - 1) * CHUNK : c * CHUNK]
+            scales = keep.tile([P, CHUNK], U8, align_bytes=64, name=f"scales{c}")
             nc.vector.quantize_mx(
                 out=codes.bitcast(FP8X4),
                 scales=scales[:],
-                in_=keys[:, lo:hi, :].rearrange("p n j -> p (n j)"),
+                in_=keys[:, slots, :].rearrange("p n j -> p (n j)"),
             )
-            acc = psum.tile([QUERIES, hi - lo], F32, name=f"acc{lo}")
+            acc = psum.tile([QUERIES, CHUNK], F32, name=f"acc{c}")
             nc.tensor.matmul_mx(
                 out=acc[:],
                 lhsT=q_codes[:].bitcast(FP8X4),
@@ -80,46 +101,8 @@ def tile_attend_sddmm_kernel(tc, qT, kT, offs, out):
                 start=True,
                 stop=True,
             )
-            return acc
+            nc.scalar.copy(result[:, slots], acc[:])
 
-        def scatter(lo, hi):
-            nc.vector.tensor_copy(listed(window, lo, hi), result[:, lo:hi])
-
-        def load(j):
-            nc.sync.dma_start(planes[j][:], k_rows[j])
-
-        load(0)
-        nc.sync.dma_start(offsets[:], offs)
-        load(1)
-        load(2)
-        load(3)
-        nc.sync.dma_start(q_raw[:], q_rows)
-        nc.vector.memset(window[:], 0.0)
-        cast_on_scalar(0, 768, 1024)
-        cast_on_vector(0, 0, 768)
-        gather_on_vector(0, 0, 160)
-        gather_on_scalar(0, 160, SLOTS)
-        cast_on_vector(1, 0, 1024)
-        gather_on_vector(1, 0, 160)
-        gather_on_scalar(1, 160, SLOTS)
-        cast_on_vector(2, 0, 1024)
-        gather_on_vector(2, 0, 128)
-        gather_on_scalar(2, 128, SLOTS)
-        cast_on_vector(3, 0, 1024)
-        gather_on_vector(3, 0, 128)
-        gather_on_scalar(3, 128, 384)
-        gather_on_scalar(3, 384, 512)
-        nc.vector.tensor_copy(q_grouped[:, 0:128, :], q_raw[:, :, 0:128].rearrange("p j q -> p q j"))
-        quantise_queries()
-        acc = quantise(0, 128, new_codes(128, "codes0")[:])
-        nc.scalar.copy(result[:, 0:128], acc[:])
-        late = keep.tile([P, 384], U32, align_bytes=64, tag="stage", name="late")
-        acc = quantise(128, 256, late[:, 0:128])
-        nc.scalar.copy(result[:, 128:256], acc[:])
-        acc = quantise(256, 384, late[:, 128:256])
-        nc.scalar.copy(result[:, 256:384], acc[:])
-        acc = quantise(384, 512, late[:, 256:384])
-        nc.scalar.copy(result[:, 384:512], acc[:])
-        scatter(0, 128)
-        scatter(128, 512)
+        for first, end in ((0, CHUNK), (CHUNK, SLOTS)):
+            nc.vector.tensor_copy(listed(window, first, end), result[:, first:end])
         nc.sync.dma_start(out[0], window[:])

@@ -7,12 +7,6 @@ P = 128
 PACK = 4
 CHUNK = 128
 OFFSETS_A_COLUMN = 16
-PLANE_ORDER = (0, 2, 3, 1)
-HALF = TOKENS // 2
-
-VECTOR_SLOTS = (192, CHUNK, 160, 160)
-VECTOR_CASTS = ((HALF, TOKENS), (0, TOKENS), (0, TOKENS), (0, TOKENS))
-LAST_CUT = 384
 
 FLOPS = 2 * QUERIES * FEATURES * SLOTS
 
@@ -23,6 +17,14 @@ U16 = mybir.dt.uint16
 U8 = mybir.dt.uint8
 FP8X4 = mybir.dt.float8_e4m3fn_x4
 COPY = mybir.ActivationFunctionType.Copy
+
+LOADS = ((0, 0, 1024), "list", (2, 0, 1024), (3, 0, 1024), (1, 0, 320), (1, 320, 1024), "queries")
+CASTS = ((("vector", 0, 768), ("scalar", 768, 1024)), (("vector", 0, 320), ("vector", 320, 1024)), (("vector", 0, 1024),), (("vector", 0, 1024),))
+GATHERS = ((("vector", 0, 224), ("scalar", 224, 512)), (("vector", 0, 128), ("scalar", 128, 384), ("scalar", 384, 512)), (("vector", 0, 192), ("scalar", 192, 512)), (("vector", 0, 160), ("scalar", 160, 512)))
+PLANE_ORDER = (0, 2, 3, 1)
+QUERIES_AFTER = 4
+CHUNKS = ((0, 128), (128, 256), (256, 384), (384, 512))
+SCATTERS = ((0, 128), (128, 512))
 
 
 def tile_attend_sddmm_kernel(tc, qT, kT, offs, out):
@@ -38,12 +40,14 @@ def tile_attend_sddmm_kernel(tc, qT, kT, offs, out):
         planes = [keep.tile([P, TOKENS], F32, name=f"plane{j}") for j in range(PACK)]
         q_raw = keep.tile([P, PACK, QUERIES], F32, name="q_raw")
 
-        nc.sync.dma_start(planes[0][:, :HALF], k_rows[0][:, :HALF])
-        nc.sync.dma_start(planes[0][:, HALF:], k_rows[0][:, HALF:])
-        nc.sync.dma_start(offsets[:], offs)
-        for j in PLANE_ORDER[1:]:
-            nc.sync.dma_start(planes[j][:], k_rows[j])
-        nc.sync.dma_start(q_raw[:], q_rows)
+        for load in LOADS:
+            if load == "list":
+                nc.sync.dma_start(offsets[:], offs)
+            elif load == "queries":
+                nc.sync.dma_start(q_raw[:], q_rows)
+            else:
+                j, first, end = load
+                nc.sync.dma_start(planes[j][:, first:end], k_rows[j][:, first:end])
 
         window = keep.tile([P, TOKENS], F32, name="window")
         nc.vector.memset(window[:], 0.0)
@@ -57,41 +61,43 @@ def tile_attend_sddmm_kernel(tc, qT, kT, offs, out):
         def listed(tile, lo, hi):
             return tile[:].indirect(offsets[:, lo // OFFSETS_A_COLUMN : hi // OFFSETS_A_COLUMN])
 
-        for j in PLANE_ORDER:
-            lo, hi = VECTOR_CASTS[j]
-            if lo > 0:
-                nc.scalar.activation(rounded[j][:, :lo], planes[j][:, :lo], COPY)
-            nc.vector.tensor_copy(rounded[j][:, lo:hi], planes[j][:, lo:hi])
-            if hi < TOKENS:
-                nc.scalar.activation(rounded[j][:, hi:], planes[j][:, hi:], COPY)
+        def move(engine, dst, src):
+            if engine == "vector":
+                nc.vector.tensor_copy(dst, src)
+            else:
+                nc.scalar.activation(dst, src, COPY)
 
-            bound = VECTOR_SLOTS[j]
-            nc.vector.tensor_copy(keys[:, :bound, j], listed(planes[j], 0, bound))
-            last_plane = j == PLANE_ORDER[-1]
-            for first, end in ((bound, LAST_CUT), (LAST_CUT, SLOTS)) if last_plane else ((bound, SLOTS),):
-                nc.scalar.activation(keys[:, first:end, j], listed(rounded[j], first, end), COPY)
+        def queries():
+            for engine, first, end in (("vector", 0, QUERIES),):
+                move(engine, q_grouped[:, first:end, :], q_raw[:, :, first:end].rearrange("p j q -> p q j"))
+            nc.vector.quantize_mx(
+                out=q_codes[:].bitcast(FP8X4),
+                scales=q_scales[:],
+                in_=q_grouped[:].rearrange("p q j -> p (q j)"),
+            )
 
-        nc.vector.tensor_copy(q_grouped[:], q_raw[:].rearrange("p j q -> p q j"))
-        nc.vector.quantize_mx(
-            out=q_codes[:].bitcast(FP8X4),
-            scales=q_scales[:],
-            in_=q_grouped[:].rearrange("p q j -> p (q j)"),
-        )
+        for done, j in enumerate(PLANE_ORDER):
+            for engine, first, end in CASTS[j]:
+                move(engine, rounded[j][:, first:end], planes[j][:, first:end])
+            for engine, first, end in GATHERS[j]:
+                source = planes[j] if engine == "vector" else rounded[j]
+                move(engine, keys[:, first:end, j], listed(source, first, end))
+            if done + 1 == QUERIES_AFTER:
+                queries()
 
-        first_codes = keep.tile([P, CHUNK], U32, align_bytes=64, name="first_codes")
-        late_codes = keep.tile([P, SLOTS - CHUNK], U32, align_bytes=64, tag="stage", name="late_codes")
+        first_codes = keep.tile([P, CHUNKS[0][1]], U32, align_bytes=64, name="first_codes")
+        late_codes = keep.tile([P, SLOTS - CHUNKS[0][1]], U32, align_bytes=64, tag="stage", name="late_codes")
         result = keep.tile([QUERIES, SLOTS], F32, name="result")
 
-        for c in range(SLOTS // CHUNK):
-            slots = slice(c * CHUNK, (c + 1) * CHUNK)
-            codes = first_codes[:] if c == 0 else late_codes[:, (c - 1) * CHUNK : c * CHUNK]
-            scales = keep.tile([P, CHUNK], U8, align_bytes=64, name=f"scales{c}")
+        for c, (first, end) in enumerate(CHUNKS):
+            codes = first_codes[:] if c == 0 else late_codes[:, first - CHUNKS[0][1] : end - CHUNKS[0][1]]
+            scales = keep.tile([P, end - first], U8, align_bytes=64, name=f"scales{c}")
             nc.vector.quantize_mx(
                 out=codes.bitcast(FP8X4),
                 scales=scales[:],
-                in_=keys[:, slots, :].rearrange("p n j -> p (n j)"),
+                in_=keys[:, first:end, :].rearrange("p n j -> p (n j)"),
             )
-            acc = psum.tile([QUERIES, CHUNK], F32, name=f"acc{c}")
+            acc = psum.tile([QUERIES, end - first], F32, name=f"acc{c}")
             nc.tensor.matmul_mx(
                 out=acc[:],
                 lhsT=q_codes[:].bitcast(FP8X4),
@@ -101,8 +107,8 @@ def tile_attend_sddmm_kernel(tc, qT, kT, offs, out):
                 start=True,
                 stop=True,
             )
-            nc.scalar.copy(result[:, slots], acc[:])
+            nc.scalar.copy(result[:, first:end], acc[:])
 
-        for first, end in ((0, CHUNK), (CHUNK, SLOTS)):
+        for first, end in SCATTERS:
             nc.vector.tensor_copy(listed(window, first, end), result[:, first:end])
         nc.sync.dma_start(out[0], window[:])

@@ -20,7 +20,7 @@ COPY = mybir.ActivationFunctionType.Copy
 
 LOADS = ((0, 0, 1024), "list", (2, 0, 1024), (3, 0, 1024), (1, 0, 320), (1, 320, 1024), "queries")
 CASTS = ((("vector", 0, 768), ("scalar", 768, 1024)), (("vector", 0, 320), ("vector", 320, 1024)), (("vector", 0, 1024),), (("vector", 0, 1024),))
-GATHERS = ((("vector", 0, 224), ("scalar", 224, 512)), (("vector", 0, 128), ("scalar", 128, 384), ("scalar", 384, 512)), (("vector", 0, 192), ("scalar", 192, 512)), (("vector", 0, 160), ("scalar", 160, 512)))
+GATHERS = ((("vector", 0, 192), ("scalar", 192, 512)), (("vector", 0, 128), ("scalar", 128, 384), ("scalar", 384, 512)), (("vector", 0, 160), ("scalar", 160, 512)), (("vector", 0, 128), ("scalar", 128, 512)))
 PLANE_ORDER = (0, 2, 3, 1)
 QUERIES_AFTER = 4
 CHUNKS = ((0, 128), (128, 256), (256, 384), (384, 512))
@@ -69,7 +69,11 @@ def tile_attend_sddmm_kernel(tc, qT, kT, offs, out):
 
         def queries():
             for engine, first, end in (("vector", 0, QUERIES),):
-                move(engine, q_grouped[:, first:end, :], q_raw[:, :, first:end].rearrange("p j q -> p q j"))
+                move(
+                    engine,
+                    q_grouped[:, first:end, :].rearrange("p (c i) j -> p c j i", i=4),
+                    q_raw[:, :, first:end].rearrange("p j (c i) -> p c j i", i=4),
+                )
             nc.vector.quantize_mx(
                 out=q_codes[:].bitcast(FP8X4),
                 scales=q_scales[:],

@@ -7,6 +7,15 @@ P = 128
 PACK = 4
 CHUNK = 128
 OFFSETS_A_COLUMN = 16
+PLANE_ORDER = (0, 2, 3, 1)
+FIRST_PLANE, LAST_PLANE = PLANE_ORDER[0], PLANE_ORDER[-1]
+
+VECTOR_SLOTS = (192, CHUNK, 160, CHUNK)
+FIRST_CAST_SPLIT = 768
+EARLY_TOKENS = 384
+LAST_GATHER_CUT = 384
+QUERY_HALF = QUERIES // 2
+NEIGHBOURS = 4
 
 FLOPS = 2 * QUERIES * FEATURES * SLOTS
 
@@ -18,19 +27,12 @@ U8 = mybir.dt.uint8
 FP8X4 = mybir.dt.float8_e4m3fn_x4
 COPY = mybir.ActivationFunctionType.Copy
 
-LOADS = ((0, 0, 1024), "list", (2, 0, 1024), (3, 0, 1024), (1, 0, 320), (1, 320, 1024), "queries")
-CASTS = ((("vector", 0, 768), ("scalar", 768, 1024)), (("vector", 0, 320), ("vector", 320, 1024)), (("vector", 0, 1024),), (("vector", 0, 1024),))
-GATHERS = ((("vector", 0, 192), ("scalar", 192, 512)), (("vector", 0, 128), ("scalar", 128, 384), ("scalar", 384, 512)), (("vector", 0, 160), ("scalar", 160, 512)), (("vector", 0, 128), ("scalar", 128, 512)))
-PLANE_ORDER = (0, 2, 3, 1)
-QUERIES_AFTER = 4
-CHUNKS = ((0, 128), (128, 256), (256, 384), (384, 512))
-SCATTERS = ((0, 128), (128, 512))
-
 
 def tile_attend_sddmm_kernel(tc, qT, kT, offs, out):
     nc = tc.nc
     k_rows = kT.rearrange("(p j) t -> j p t", j=PACK)
     q_rows = qT[0].rearrange("(p j) q -> p j q", j=PACK)
+    last_pieces = (slice(0, EARLY_TOKENS), slice(EARLY_TOKENS, TOKENS))
 
     with ExitStack() as ctx:
         keep = ctx.enter_context(tc.tile_pool(name="keep", bufs=1))
@@ -40,14 +42,13 @@ def tile_attend_sddmm_kernel(tc, qT, kT, offs, out):
         planes = [keep.tile([P, TOKENS], F32, name=f"plane{j}") for j in range(PACK)]
         q_raw = keep.tile([P, PACK, QUERIES], F32, name="q_raw")
 
-        for load in LOADS:
-            if load == "list":
-                nc.sync.dma_start(offsets[:], offs)
-            elif load == "queries":
-                nc.sync.dma_start(q_raw[:], q_rows)
-            else:
-                j, first, end = load
-                nc.sync.dma_start(planes[j][:, first:end], k_rows[j][:, first:end])
+        nc.sync.dma_start(planes[FIRST_PLANE][:], k_rows[FIRST_PLANE])
+        nc.sync.dma_start(offsets[:], offs)
+        for j in PLANE_ORDER[1:-1]:
+            nc.sync.dma_start(planes[j][:], k_rows[j])
+        for piece in last_pieces:
+            nc.sync.dma_start(planes[LAST_PLANE][:, piece], k_rows[LAST_PLANE][:, piece])
+        nc.sync.dma_start(q_raw[:], q_rows)
 
         window = keep.tile([P, TOKENS], F32, name="window")
         nc.vector.memset(window[:], 0.0)
@@ -58,50 +59,52 @@ def tile_attend_sddmm_kernel(tc, qT, kT, offs, out):
         q_codes = keep.tile([P, QUERIES], U32, align_bytes=64, name="q_codes")
         q_scales = keep.tile([P, QUERIES], U8, align_bytes=64, name="q_scales")
 
-        def listed(tile, lo, hi):
-            return tile[:].indirect(offsets[:, lo // OFFSETS_A_COLUMN : hi // OFFSETS_A_COLUMN])
+        def listed(tile, first, end):
+            return tile[:].indirect(offsets[:, first // OFFSETS_A_COLUMN : end // OFFSETS_A_COLUMN])
 
-        def move(engine, dst, src):
-            if engine == "vector":
-                nc.vector.tensor_copy(dst, src)
+        for j in PLANE_ORDER:
+            if j == FIRST_PLANE:
+                nc.vector.tensor_copy(rounded[j][:, :FIRST_CAST_SPLIT], planes[j][:, :FIRST_CAST_SPLIT])
+                nc.scalar.activation(rounded[j][:, FIRST_CAST_SPLIT:], planes[j][:, FIRST_CAST_SPLIT:], COPY)
+            elif j == LAST_PLANE:
+                for piece in last_pieces:
+                    nc.vector.tensor_copy(rounded[j][:, piece], planes[j][:, piece])
             else:
-                nc.scalar.activation(dst, src, COPY)
+                nc.vector.tensor_copy(rounded[j][:], planes[j][:])
 
-        def queries():
-            for engine, first, end in (("vector", 0, QUERIES),):
-                move(
-                    engine,
-                    q_grouped[:, first:end, :].rearrange("p (c i) j -> p c j i", i=4),
-                    q_raw[:, :, first:end].rearrange("p j (c i) -> p c j i", i=4),
-                )
+            bound = VECTOR_SLOTS[j]
+            nc.vector.tensor_copy(keys[:, :bound, j], listed(planes[j], 0, bound))
+            cuts = (bound, LAST_GATHER_CUT, SLOTS) if j == LAST_PLANE else (bound, SLOTS)
+            for first, end in zip(cuts, cuts[1:]):
+                nc.scalar.activation(keys[:, first:end, j], listed(rounded[j], first, end), COPY)
+
+        halves = (slice(0, QUERY_HALF), slice(QUERY_HALF, QUERIES))
+        for half in halves:
+            nc.vector.tensor_copy(
+                q_grouped[:, half, :].rearrange("p (c i) j -> p c j i", i=NEIGHBOURS),
+                q_raw[:, :, half].rearrange("p j (c i) -> p c j i", i=NEIGHBOURS),
+            )
+        for half in halves:
             nc.vector.quantize_mx(
-                out=q_codes[:].bitcast(FP8X4),
-                scales=q_scales[:],
-                in_=q_grouped[:].rearrange("p q j -> p (q j)"),
+                out=q_codes[:, half].bitcast(FP8X4),
+                scales=q_scales[:, half],
+                in_=q_grouped[:, half, :].rearrange("p q j -> p (q j)"),
             )
 
-        for done, j in enumerate(PLANE_ORDER):
-            for engine, first, end in CASTS[j]:
-                move(engine, rounded[j][:, first:end], planes[j][:, first:end])
-            for engine, first, end in GATHERS[j]:
-                source = planes[j] if engine == "vector" else rounded[j]
-                move(engine, keys[:, first:end, j], listed(source, first, end))
-            if done + 1 == QUERIES_AFTER:
-                queries()
-
-        first_codes = keep.tile([P, CHUNKS[0][1]], U32, align_bytes=64, name="first_codes")
-        late_codes = keep.tile([P, SLOTS - CHUNKS[0][1]], U32, align_bytes=64, tag="stage", name="late_codes")
+        first_codes = keep.tile([P, CHUNK], U32, align_bytes=64, name="first_codes")
+        late_codes = keep.tile([P, SLOTS - CHUNK], U32, align_bytes=64, tag="stage", name="late_codes")
         result = keep.tile([QUERIES, SLOTS], F32, name="result")
 
-        for c, (first, end) in enumerate(CHUNKS):
-            codes = first_codes[:] if c == 0 else late_codes[:, first - CHUNKS[0][1] : end - CHUNKS[0][1]]
-            scales = keep.tile([P, end - first], U8, align_bytes=64, name=f"scales{c}")
+        for c in range(SLOTS // CHUNK):
+            slots = slice(c * CHUNK, (c + 1) * CHUNK)
+            codes = first_codes[:] if c == 0 else late_codes[:, (c - 1) * CHUNK : c * CHUNK]
+            scales = keep.tile([P, CHUNK], U8, align_bytes=64, name=f"scales{c}")
             nc.vector.quantize_mx(
                 out=codes.bitcast(FP8X4),
                 scales=scales[:],
-                in_=keys[:, first:end, :].rearrange("p n j -> p (n j)"),
+                in_=keys[:, slots, :].rearrange("p n j -> p (n j)"),
             )
-            acc = psum.tile([QUERIES, end - first], F32, name=f"acc{c}")
+            acc = psum.tile([QUERIES, CHUNK], F32, name=f"acc{c}")
             nc.tensor.matmul_mx(
                 out=acc[:],
                 lhsT=q_codes[:].bitcast(FP8X4),
@@ -111,8 +114,8 @@ def tile_attend_sddmm_kernel(tc, qT, kT, offs, out):
                 start=True,
                 stop=True,
             )
-            nc.scalar.copy(result[:, first:end], acc[:])
+            nc.scalar.copy(result[:, slots], acc[:])
 
-        for first, end in SCATTERS:
+        for first, end in ((0, CHUNK), (CHUNK, SLOTS)):
             nc.vector.tensor_copy(listed(window, first, end), result[:, first:end])
         nc.sync.dma_start(out[0], window[:])

@@ -7,14 +7,6 @@ P = 128
 PACK = 4
 CHUNK = 128
 OFFSETS_A_COLUMN = 16
-PLANE_ORDER = (0, 2, 3, 1)
-FIRST_PLANE, LAST_PLANE = PLANE_ORDER[0], PLANE_ORDER[-1]
-
-VECTOR_SLOTS = (192, CHUNK, 160, CHUNK)
-FIRST_CAST_SPLIT = 768
-EARLY_TOKENS = 384
-LAST_GATHER_CUT = 384
-QUERY_HALF = QUERIES // 2
 NEIGHBOURS = 4
 
 FLOPS = 2 * QUERIES * FEATURES * SLOTS
@@ -27,12 +19,14 @@ U8 = mybir.dt.uint8
 FP8X4 = mybir.dt.float8_e4m3fn_x4
 COPY = mybir.ActivationFunctionType.Copy
 
+SCALAR_SCATTER = 320
+
 
 def tile_attend_sddmm_kernel(tc, qT, kT, offs, out):
     nc = tc.nc
     k_rows = kT.rearrange("(p j) t -> j p t", j=PACK)
     q_rows = qT[0].rearrange("(p j) q -> p j q", j=PACK)
-    last_pieces = (slice(0, EARLY_TOKENS), slice(EARLY_TOKENS, TOKENS))
+    chunks = [slice(c * CHUNK, (c + 1) * CHUNK) for c in range(SLOTS // CHUNK)]
 
     with ExitStack() as ctx:
         keep = ctx.enter_context(tc.tile_pool(name="keep", bufs=1))
@@ -42,80 +36,66 @@ def tile_attend_sddmm_kernel(tc, qT, kT, offs, out):
         planes = [keep.tile([P, TOKENS], F32, name=f"plane{j}") for j in range(PACK)]
         q_raw = keep.tile([P, PACK, QUERIES], F32, name="q_raw")
 
-        nc.sync.dma_start(planes[FIRST_PLANE][:], k_rows[FIRST_PLANE])
-        nc.sync.dma_start(offsets[:], offs)
-        for j in PLANE_ORDER[1:-1]:
-            nc.sync.dma_start(planes[j][:], k_rows[j])
-        for piece in last_pieces:
-            nc.sync.dma_start(planes[LAST_PLANE][:, piece], k_rows[LAST_PLANE][:, piece])
         nc.sync.dma_start(q_raw[:], q_rows)
+        nc.sync.dma_start(offsets[:], offs)
+        for j in range(PACK):
+            nc.sync.dma_start(planes[j][:], k_rows[j])
 
-        window = keep.tile([P, TOKENS], F32, name="window")
-        nc.vector.memset(window[:], 0.0)
+        windows = [keep.tile([P, TOKENS], F32, name=f"window{w}") for w in range(2)]
+        for window in windows:
+            nc.vector.memset(window[:], 0.0)
 
-        rounded = [keep.tile([P, TOKENS], BF16, name=f"rounded{j}") for j in range(PACK)]
         keys = keep.tile([P, SLOTS, PACK], BF16, align_bytes=64, name="keys")
-        q_grouped = keep.tile([P, QUERIES, PACK], BF16, align_bytes=64, tag="stage", name="q_grouped")
+        early = keep.tile([P, 2, SLOTS - CHUNK], BF16, name="early")
+        late = [keep.tile([P, 2, CHUNK], BF16, name=f"late{c}") for c in range(1, len(chunks))]
+        q_grouped = keep.tile([P, QUERIES, PACK], BF16, align_bytes=64, name="q_grouped")
         q_codes = keep.tile([P, QUERIES], U32, align_bytes=64, name="q_codes")
         q_scales = keep.tile([P, QUERIES], U8, align_bytes=64, name="q_scales")
 
         def listed(tile, first, end):
             return tile[:].indirect(offsets[:, first // OFFSETS_A_COLUMN : end // OFFSETS_A_COLUMN])
 
-        for j in PLANE_ORDER:
-            if j == FIRST_PLANE:
-                nc.vector.tensor_copy(rounded[j][:, :FIRST_CAST_SPLIT], planes[j][:, :FIRST_CAST_SPLIT])
-                nc.scalar.activation(rounded[j][:, FIRST_CAST_SPLIT:], planes[j][:, FIRST_CAST_SPLIT:], COPY)
-            elif j == LAST_PLANE:
-                for piece in last_pieces:
-                    nc.vector.tensor_copy(rounded[j][:, piece], planes[j][:, piece])
+        nc.scalar.activation(q_grouped[:], q_raw[:].rearrange("p j q -> p q j"), COPY)
+        nc.vector.quantize_mx(
+            out=q_codes[:].bitcast(FP8X4), scales=q_scales[:], in_=q_grouped[:].rearrange("p q j -> p (q j)")
+        )
+        for j in range(PACK):
+            nc.vector.tensor_copy(keys[:, :CHUNK, j], listed(planes[j], 0, CHUNK))
+            if j < 2:
+                nc.scalar.activation(early[:, j, :], listed(planes[j], CHUNK, SLOTS), COPY)
             else:
-                nc.vector.tensor_copy(rounded[j][:], planes[j][:])
+                for slots, tile in zip(chunks[1:], late):
+                    nc.scalar.activation(tile[:, j - 2, :], listed(planes[j], slots.start, slots.stop), COPY)
+            if j == 1:
+                nc.vector.tensor_copy(keys[:, CHUNK:, 0:2], early[:].rearrange("p j n -> p n j"))
 
-            bound = VECTOR_SLOTS[j]
-            nc.vector.tensor_copy(keys[:, :bound, j], listed(planes[j], 0, bound))
-            cuts = (bound, LAST_GATHER_CUT, SLOTS) if j == LAST_PLANE else (bound, SLOTS)
-            for first, end in zip(cuts, cuts[1:]):
-                nc.scalar.activation(keys[:, first:end, j], listed(rounded[j], first, end), COPY)
-
-        halves = (slice(0, QUERY_HALF), slice(QUERY_HALF, QUERIES))
-        for half in halves:
-            nc.vector.tensor_copy(
-                q_grouped[:, half, :].rearrange("p (c i) j -> p c j i", i=NEIGHBOURS),
-                q_raw[:, :, half].rearrange("p j (c i) -> p c j i", i=NEIGHBOURS),
-            )
-        for half in halves:
-            nc.vector.quantize_mx(
-                out=q_codes[:, half].bitcast(FP8X4),
-                scales=q_scales[:, half],
-                in_=q_grouped[:, half, :].rearrange("p q j -> p (q j)"),
-            )
-
-        first_codes = keep.tile([P, CHUNK], U32, align_bytes=64, name="first_codes")
-        late_codes = keep.tile([P, SLOTS - CHUNK], U32, align_bytes=64, tag="stage", name="late_codes")
         result = keep.tile([QUERIES, SLOTS], F32, name="result")
-
-        for c in range(SLOTS // CHUNK):
-            slots = slice(c * CHUNK, (c + 1) * CHUNK)
-            codes = first_codes[:] if c == 0 else late_codes[:, (c - 1) * CHUNK : c * CHUNK]
+        banks = [psum.tile([QUERIES, CHUNK], F32, name=f"acc{c}") for c in range(len(chunks))]
+        for c, slots in enumerate(chunks):
+            if c + 1 < len(chunks):
+                nc.vector.tensor_copy(keys[:, chunks[c + 1], 2:4], late[c][:].rearrange("p j n -> p n j"))
+            codes = keep.tile([P, CHUNK], U32, align_bytes=64, name=f"codes{c}")
             scales = keep.tile([P, CHUNK], U8, align_bytes=64, name=f"scales{c}")
             nc.vector.quantize_mx(
-                out=codes.bitcast(FP8X4),
-                scales=scales[:],
-                in_=keys[:, slots, :].rearrange("p n j -> p (n j)"),
+                out=codes[:].bitcast(FP8X4), scales=scales[:], in_=keys[:, slots, :].rearrange("p n j -> p (n j)")
             )
-            acc = psum.tile([QUERIES, CHUNK], F32, name=f"acc{c}")
             nc.tensor.matmul_mx(
-                out=acc[:],
+                out=banks[c][:],
                 lhsT=q_codes[:].bitcast(FP8X4),
                 lhsT_scale=q_scales[:],
-                rhs=codes.bitcast(FP8X4),
+                rhs=codes[:].bitcast(FP8X4),
                 rhs_scale=scales[:],
                 start=True,
                 stop=True,
             )
-            nc.scalar.copy(result[:, slots], acc[:])
+        nc.scalar.copy(result[:, chunks[0]], banks[0][:])
+        for c in range(1, len(chunks)):
+            nc.vector.tensor_copy(result[:, chunks[c]], banks[c][:])
 
-        for first, end in ((0, CHUNK), (CHUNK, SLOTS)):
-            nc.vector.tensor_copy(listed(window, first, end), result[:, first:end])
-        nc.sync.dma_start(out[0], window[:])
+        for first, end in ((0, CHUNK), (CHUNK, SCALAR_SCATTER)):
+            nc.scalar.activation(listed(windows[0], first, end), result[:, first:end], COPY)
+        nc.vector.tensor_copy(listed(windows[1], SCALAR_SCATTER, SLOTS), result[:, SCALAR_SCATTER:])
+        total = keep.tile([P, TOKENS], F32, name="total")
+        for piece in (slice(0, TOKENS // 2), slice(TOKENS // 2, TOKENS)):
+            nc.vector.tensor_add(total[:, piece], windows[0][:, piece], windows[1][:, piece])
+            nc.sync.dma_start(out[0][:, piece], total[:, piece])

@@ -19,7 +19,9 @@ U8 = mybir.dt.uint8
 FP8X4 = mybir.dt.float8_e4m3fn_x4
 COPY = mybir.ActivationFunctionType.Copy
 
-SCALAR_SCATTER = 320
+VECTOR_SLOTS = 256
+SCATTER_CUT = 352
+STORE_PIECES = 2
 
 
 def tile_attend_sddmm_kernel(tc, qT, kT, offs, out):
@@ -27,6 +29,7 @@ def tile_attend_sddmm_kernel(tc, qT, kT, offs, out):
     k_rows = kT.rearrange("(p j) t -> j p t", j=PACK)
     q_rows = qT[0].rearrange("(p j) q -> p j q", j=PACK)
     chunks = [slice(c * CHUNK, (c + 1) * CHUNK) for c in range(SLOTS // CHUNK)]
+    scalar_parts = [slice(max(s.start, VECTOR_SLOTS), s.stop) for s in chunks[2:]]
 
     with ExitStack() as ctx:
         keep = ctx.enter_context(tc.tile_pool(name="keep", bufs=1))
@@ -46,8 +49,8 @@ def tile_attend_sddmm_kernel(tc, qT, kT, offs, out):
             nc.vector.memset(window[:], 0.0)
 
         keys = keep.tile([P, SLOTS, PACK], BF16, align_bytes=64, name="keys")
-        early = keep.tile([P, 2, SLOTS - CHUNK], BF16, name="early")
-        late = [keep.tile([P, 2, CHUNK], BF16, name=f"late{c}") for c in range(1, len(chunks))]
+        early = keep.tile([P, 2, SLOTS - VECTOR_SLOTS], BF16, name="early")
+        late = [keep.tile([P, 2, s.stop - s.start], BF16, name=f"late{s.start}") for s in scalar_parts]
         q_grouped = keep.tile([P, QUERIES, PACK], BF16, align_bytes=64, name="q_grouped")
         q_codes = keep.tile([P, QUERIES], U32, align_bytes=64, name="q_codes")
         q_scales = keep.tile([P, QUERIES], U8, align_bytes=64, name="q_scales")
@@ -60,20 +63,24 @@ def tile_attend_sddmm_kernel(tc, qT, kT, offs, out):
             out=q_codes[:].bitcast(FP8X4), scales=q_scales[:], in_=q_grouped[:].rearrange("p q j -> p (q j)")
         )
         for j in range(PACK):
-            nc.vector.tensor_copy(keys[:, :CHUNK, j], listed(planes[j], 0, CHUNK))
+            cuts = (0, CHUNK, VECTOR_SLOTS) if j == PACK - 1 else (0, VECTOR_SLOTS)
+            for first, end in zip(cuts, cuts[1:]):
+                if end > first:
+                    nc.vector.tensor_copy(keys[:, first:end, j], listed(planes[j], first, end))
             if j < 2:
-                nc.scalar.activation(early[:, j, :], listed(planes[j], CHUNK, SLOTS), COPY)
+                nc.scalar.activation(early[:, j, :], listed(planes[j], VECTOR_SLOTS, SLOTS), COPY)
             else:
-                for slots, tile in zip(chunks[1:], late):
+                for slots, tile in zip(scalar_parts, late):
                     nc.scalar.activation(tile[:, j - 2, :], listed(planes[j], slots.start, slots.stop), COPY)
             if j == 1:
-                nc.vector.tensor_copy(keys[:, CHUNK:, 0:2], early[:].rearrange("p j n -> p n j"))
+                nc.vector.tensor_copy(keys[:, VECTOR_SLOTS:, 0:2], early[:].rearrange("p j n -> p n j"))
 
         result = keep.tile([QUERIES, SLOTS], F32, name="result")
         banks = [psum.tile([QUERIES, CHUNK], F32, name=f"acc{c}") for c in range(len(chunks))]
+        nc.scalar.activation(keys[:, chunks[2], 2:4], late[0][:].rearrange("p j n -> p n j"), COPY)
         for c, slots in enumerate(chunks):
-            if c + 1 < len(chunks):
-                nc.vector.tensor_copy(keys[:, chunks[c + 1], 2:4], late[c][:].rearrange("p j n -> p n j"))
+            if c == 1:
+                nc.vector.tensor_copy(keys[:, chunks[3], 2:4], late[1][:].rearrange("p j n -> p n j"))
             codes = keep.tile([P, CHUNK], U32, align_bytes=64, name=f"codes{c}")
             scales = keep.tile([P, CHUNK], U8, align_bytes=64, name=f"scales{c}")
             nc.vector.quantize_mx(
@@ -89,13 +96,15 @@ def tile_attend_sddmm_kernel(tc, qT, kT, offs, out):
                 stop=True,
             )
         nc.scalar.copy(result[:, chunks[0]], banks[0][:])
-        for c in range(1, len(chunks)):
+        nc.scalar.activation(listed(windows[0], 0, CHUNK), result[:, :CHUNK], COPY)
+        for c in (1, 2):
             nc.vector.tensor_copy(result[:, chunks[c]], banks[c][:])
-
-        for first, end in ((0, CHUNK), (CHUNK, SCALAR_SCATTER)):
-            nc.scalar.activation(listed(windows[0], first, end), result[:, first:end], COPY)
-        nc.vector.tensor_copy(listed(windows[1], SCALAR_SCATTER, SLOTS), result[:, SCALAR_SCATTER:])
+        nc.vector.tensor_copy(result[:, chunks[3]], banks[3][:])
+        nc.vector.tensor_copy(listed(windows[1], CHUNK, SCATTER_CUT), result[:, CHUNK:SCATTER_CUT])
+        nc.scalar.activation(listed(windows[0], SCATTER_CUT, SLOTS), result[:, SCATTER_CUT:], COPY)
         total = keep.tile([P, TOKENS], F32, name="total")
-        for piece in (slice(0, TOKENS // 2), slice(TOKENS // 2, TOKENS)):
+        width = TOKENS // STORE_PIECES
+        for first in range(0, TOKENS, width):
+            piece = slice(first, first + width)
             nc.vector.tensor_add(total[:, piece], windows[0][:, piece], windows[1][:, piece])
             nc.sync.dma_start(out[0][:, piece], total[:, piece])

@@ -7,7 +7,6 @@ P = 128
 PACK = 4
 CHUNK = 128
 OFFSETS_A_COLUMN = 16
-NEIGHBOURS = 4
 
 FLOPS = 2 * QUERIES * FEATURES * SLOTS
 
@@ -19,30 +18,42 @@ U8 = mybir.dt.uint8
 FP8X4 = mybir.dt.float8_e4m3fn_x4
 COPY = mybir.ActivationFunctionType.Copy
 
-VECTOR_SLOTS = 256
-SCATTER_CUT = 352
+VECTOR_SLOTS = 192
+VECTOR_LAYS = 128
+NEIGHBOURS = 4
+SCATTER_CUT = 384
 STORE_PIECES = 2
 
 
 def tile_attend_sddmm_kernel(tc, qT, kT, offs, out):
     nc = tc.nc
     k_rows = kT.rearrange("(p j) t -> j p t", j=PACK)
-    q_rows = qT[0].rearrange("(p j) q -> p j q", j=PACK)
+    q_rows = qT[0].rearrange("(p j) q -> p (j q)", j=PACK)
     chunks = [slice(c * CHUNK, (c + 1) * CHUNK) for c in range(SLOTS // CHUNK)]
-    scalar_parts = [slice(max(s.start, VECTOR_SLOTS), s.stop) for s in chunks[2:]]
+    laid = slice(VECTOR_SLOTS, VECTOR_SLOTS + VECTOR_LAYS)
+    scalar_parts = [laid, slice(laid.stop, chunks[2].stop), chunks[3]]
 
     with ExitStack() as ctx:
         keep = ctx.enter_context(tc.tile_pool(name="keep", bufs=1))
+        reuse = ctx.enter_context(tc.tile_pool(name="reuse", bufs=1))
         psum = ctx.enter_context(tc.psum_pool(name="psum", bufs=1))
 
         offsets = keep.tile([P, SLOTS // OFFSETS_A_COLUMN], U16, name="offsets")
         planes = [keep.tile([P, TOKENS], F32, name=f"plane{j}") for j in range(PACK)]
-        q_raw = keep.tile([P, PACK, QUERIES], F32, name="q_raw")
+        row_words = VECTOR_LAYS // 2
+        staged = reuse.tile([P, 2, row_words + PACK * QUERIES], F32, align_bytes=64, offset=0, name="staged")
+        q_raw = staged[:, 0, row_words:]
 
-        nc.sync.dma_start(q_raw[:], q_rows)
+        nc.sync.dma_start(planes[0][:], k_rows[0])
         nc.sync.dma_start(offsets[:], offs)
-        for j in range(PACK):
+        for j in range(1, PACK):
             nc.sync.dma_start(planes[j][:], k_rows[j])
+        nc.sync.dma_start(q_raw, q_rows)
+
+        warm_in = keep.tile([P, 1], F32, name="warm_in")
+        warm_out = keep.tile([P, 1], F32, name="warm_out")
+        nc.gpsimd.memset(warm_in[:], 0.0)
+        nc.scalar.activation(warm_out[:], warm_in[:], COPY)
 
         windows = [keep.tile([P, TOKENS], F32, name=f"window{w}") for w in range(2)]
         for window in windows:
@@ -50,7 +61,8 @@ def tile_attend_sddmm_kernel(tc, qT, kT, offs, out):
 
         keys = keep.tile([P, SLOTS, PACK], BF16, align_bytes=64, name="keys")
         early = keep.tile([P, 2, SLOTS - VECTOR_SLOTS], BF16, name="early")
-        late = [keep.tile([P, 2, s.stop - s.start], BF16, name=f"late{s.start}") for s in scalar_parts]
+        late = [staged[:, :, :row_words].bitcast(BF16)]
+        late.extend(keep.tile([P, 2, s.stop - s.start], BF16, name=f"late{s.start}")[:] for s in scalar_parts[1:])
         q_grouped = keep.tile([P, QUERIES, PACK], BF16, align_bytes=64, name="q_grouped")
         q_codes = keep.tile([P, QUERIES], U32, align_bytes=64, name="q_codes")
         q_scales = keep.tile([P, QUERIES], U8, align_bytes=64, name="q_scales")
@@ -58,15 +70,11 @@ def tile_attend_sddmm_kernel(tc, qT, kT, offs, out):
         def listed(tile, first, end):
             return tile[:].indirect(offsets[:, first // OFFSETS_A_COLUMN : end // OFFSETS_A_COLUMN])
 
-        nc.scalar.activation(q_grouped[:], q_raw[:].rearrange("p j q -> p q j"), COPY)
-        nc.vector.quantize_mx(
-            out=q_codes[:].bitcast(FP8X4), scales=q_scales[:], in_=q_grouped[:].rearrange("p q j -> p (q j)")
-        )
+        def quantise(codes, scales, grouped):
+            nc.vector.quantize_mx(out=codes.bitcast(FP8X4), scales=scales, in_=grouped.rearrange("p n j -> p (n j)"))
+
         for j in range(PACK):
-            cuts = (0, CHUNK, VECTOR_SLOTS) if j == PACK - 1 else (0, VECTOR_SLOTS)
-            for first, end in zip(cuts, cuts[1:]):
-                if end > first:
-                    nc.vector.tensor_copy(keys[:, first:end, j], listed(planes[j], first, end))
+            nc.vector.tensor_copy(keys[:, :VECTOR_SLOTS, j], listed(planes[j], 0, VECTOR_SLOTS))
             if j < 2:
                 nc.scalar.activation(early[:, j, :], listed(planes[j], VECTOR_SLOTS, SLOTS), COPY)
             else:
@@ -75,19 +83,25 @@ def tile_attend_sddmm_kernel(tc, qT, kT, offs, out):
             if j == 1:
                 nc.vector.tensor_copy(keys[:, VECTOR_SLOTS:, 0:2], early[:].rearrange("p j n -> p n j"))
 
+        for slots, tile in zip(scalar_parts[1:], late[1:]):
+            nc.scalar.activation(keys[:, slots, 2:4], tile.rearrange("p j n -> p n j"), COPY)
+
+        nc.vector.tensor_copy(
+            q_grouped[:].rearrange("p (c i) j -> p c j i", i=NEIGHBOURS),
+            q_raw.rearrange("p (j c i) -> p c j i", j=PACK, i=NEIGHBOURS),
+        )
+        nc.vector.tensor_copy(keys[:, laid, 2:4], late[0].rearrange("p j n -> p n j"))
+        quantise(q_codes[:], q_scales[:], q_grouped[:])
+
         result = keep.tile([QUERIES, SLOTS], F32, name="result")
         banks = [psum.tile([QUERIES, CHUNK], F32, name=f"acc{c}") for c in range(len(chunks))]
-        nc.scalar.activation(keys[:, chunks[2], 2:4], late[0][:].rearrange("p j n -> p n j"), COPY)
         for c, slots in enumerate(chunks):
-            if c == 1:
-                nc.vector.tensor_copy(keys[:, chunks[3], 2:4], late[1][:].rearrange("p j n -> p n j"))
-            codes = keep.tile([P, CHUNK], U32, align_bytes=64, name=f"codes{c}")
+            codes = reuse.tile([P, CHUNK], U32, align_bytes=64, offset=4 * CHUNK * c, name=f"codes{c}")
             scales = keep.tile([P, CHUNK], U8, align_bytes=64, name=f"scales{c}")
-            nc.vector.quantize_mx(
-                out=codes[:].bitcast(FP8X4), scales=scales[:], in_=keys[:, slots, :].rearrange("p n j -> p (n j)")
-            )
+            quantise(codes[:], scales[:], keys[:, slots, :])
+            bank = banks[c]
             nc.tensor.matmul_mx(
-                out=banks[c][:],
+                out=bank[:],
                 lhsT=q_codes[:].bitcast(FP8X4),
                 lhsT_scale=q_scales[:],
                 rhs=codes[:].bitcast(FP8X4),
@@ -95,11 +109,11 @@ def tile_attend_sddmm_kernel(tc, qT, kT, offs, out):
                 start=True,
                 stop=True,
             )
-        nc.scalar.copy(result[:, chunks[0]], banks[0][:])
+            if c < 2:
+                nc.scalar.copy(result[:, slots], bank[:])
         nc.scalar.activation(listed(windows[0], 0, CHUNK), result[:, :CHUNK], COPY)
-        for c in (1, 2):
-            nc.vector.tensor_copy(result[:, chunks[c]], banks[c][:])
-        nc.vector.tensor_copy(result[:, chunks[3]], banks[3][:])
+        for bank, slots in zip(banks[2:], chunks[2:]):
+            nc.vector.tensor_copy(result[:, slots], bank[:])
         nc.vector.tensor_copy(listed(windows[1], CHUNK, SCATTER_CUT), result[:, CHUNK:SCATTER_CUT])
         nc.scalar.activation(listed(windows[0], SCATTER_CUT, SLOTS), result[:, SCATTER_CUT:], COPY)
         total = keep.tile([P, TOKENS], F32, name="total")

@@ -18,8 +18,9 @@ U8 = mybir.dt.uint8
 FP8X4 = mybir.dt.float8_e4m3fn_x4
 COPY = mybir.ActivationFunctionType.Copy
 
-VECTOR_SLOTS = 192
-VECTOR_LAYS = 128
+VECTOR_SLOTS = 160
+VECTOR_LAYS = 160
+EARLY_CUT = 256
 NEIGHBOURS = 4
 SCATTER_CUT = 384
 STORE_PIECES = 2
@@ -59,13 +60,15 @@ def tile_attend_sddmm_kernel(tc, qT, kT, offs, out):
         for window in windows:
             nc.vector.memset(window[:], 0.0)
 
-        keys = keep.tile([P, SLOTS, PACK], BF16, align_bytes=64, name="keys")
-        early = keep.tile([P, 2, SLOTS - VECTOR_SLOTS], BF16, name="early")
+        grouped = keep.tile([P, QUERIES + SLOTS, PACK], BF16, align_bytes=64, name="grouped")
+        q_grouped, keys = grouped[:, :QUERIES, :], grouped[:, QUERIES:, :]
+        early_parts = [slice(EARLY_CUT, SLOTS), slice(VECTOR_SLOTS, EARLY_CUT)]
+        early = [keep.tile([P, 2, s.stop - s.start], BF16, name=f"early{s.start}") for s in early_parts]
         late = [staged[:, :, :row_words].bitcast(BF16)]
         late.extend(keep.tile([P, 2, s.stop - s.start], BF16, name=f"late{s.start}")[:] for s in scalar_parts[1:])
-        q_grouped = keep.tile([P, QUERIES, PACK], BF16, align_bytes=64, name="q_grouped")
-        q_codes = keep.tile([P, QUERIES], U32, align_bytes=64, name="q_codes")
-        q_scales = keep.tile([P, QUERIES], U8, align_bytes=64, name="q_scales")
+        first_codes = keep.tile([P, QUERIES + CHUNK], U32, align_bytes=64, name="first_codes")
+        first_scales = keep.tile([P, QUERIES + CHUNK], U8, align_bytes=64, name="first_scales")
+        q_codes, q_scales = first_codes[:, :QUERIES], first_scales[:, :QUERIES]
 
         def listed(tile, first, end):
             return tile[:].indirect(offsets[:, first // OFFSETS_A_COLUMN : end // OFFSETS_A_COLUMN])
@@ -76,36 +79,41 @@ def tile_attend_sddmm_kernel(tc, qT, kT, offs, out):
         for j in range(PACK):
             nc.vector.tensor_copy(keys[:, :VECTOR_SLOTS, j], listed(planes[j], 0, VECTOR_SLOTS))
             if j < 2:
-                nc.scalar.activation(early[:, j, :], listed(planes[j], VECTOR_SLOTS, SLOTS), COPY)
+                nc.scalar.activation(early[0][:, j, :], listed(planes[j], EARLY_CUT, SLOTS), COPY)
+                nc.vector.tensor_copy(early[1][:, j, :], listed(planes[j], VECTOR_SLOTS, EARLY_CUT))
             else:
                 for slots, tile in zip(scalar_parts, late):
                     nc.scalar.activation(tile[:, j - 2, :], listed(planes[j], slots.start, slots.stop), COPY)
             if j == 1:
-                nc.vector.tensor_copy(keys[:, VECTOR_SLOTS:, 0:2], early[:].rearrange("p j n -> p n j"))
+                for slots, tile in zip(early_parts, early):
+                    nc.vector.tensor_copy(keys[:, slots, 0:2], tile[:].rearrange("p j n -> p n j"))
 
         for slots, tile in zip(scalar_parts[1:], late[1:]):
             nc.scalar.activation(keys[:, slots, 2:4], tile.rearrange("p j n -> p n j"), COPY)
 
         nc.vector.tensor_copy(
-            q_grouped[:].rearrange("p (c i) j -> p c j i", i=NEIGHBOURS),
+            q_grouped.rearrange("p (c i) j -> p c j i", i=NEIGHBOURS),
             q_raw.rearrange("p (j c i) -> p c j i", j=PACK, i=NEIGHBOURS),
         )
         nc.vector.tensor_copy(keys[:, laid, 2:4], late[0].rearrange("p j n -> p n j"))
-        quantise(q_codes[:], q_scales[:], q_grouped[:])
+        quantise(first_codes[:], first_scales[:], grouped[:, : QUERIES + CHUNK, :])
 
         result = keep.tile([QUERIES, SLOTS], F32, name="result")
         banks = [psum.tile([QUERIES, CHUNK], F32, name=f"acc{c}") for c in range(len(chunks))]
         for c, slots in enumerate(chunks):
-            codes = reuse.tile([P, CHUNK], U32, align_bytes=64, offset=4 * CHUNK * c, name=f"codes{c}")
-            scales = keep.tile([P, CHUNK], U8, align_bytes=64, name=f"scales{c}")
-            quantise(codes[:], scales[:], keys[:, slots, :])
+            if c == 0:
+                codes, scales = first_codes[:, QUERIES:], first_scales[:, QUERIES:]
+            else:
+                codes = reuse.tile([P, CHUNK], U32, align_bytes=64, offset=4 * CHUNK * c, name=f"codes{c}")[:]
+                scales = keep.tile([P, CHUNK], U8, align_bytes=64, name=f"scales{c}")[:]
+                quantise(codes, scales, keys[:, slots, :])
             bank = banks[c]
             nc.tensor.matmul_mx(
                 out=bank[:],
-                lhsT=q_codes[:].bitcast(FP8X4),
-                lhsT_scale=q_scales[:],
-                rhs=codes[:].bitcast(FP8X4),
-                rhs_scale=scales[:],
+                lhsT=q_codes.bitcast(FP8X4),
+                lhsT_scale=q_scales,
+                rhs=codes.bitcast(FP8X4),
+                rhs_scale=scales,
                 start=True,
                 stop=True,
             )

@@ -20,7 +20,6 @@ COPY = mybir.ActivationFunctionType.Copy
 
 VECTOR_SLOTS = 160
 VECTOR_LAYS = 160
-EARLY_CUT = 256
 NEIGHBOURS = 4
 SCATTER_CUT = 384
 STORE_PIECES = 2
@@ -62,8 +61,7 @@ def tile_attend_sddmm_kernel(tc, qT, kT, offs, out):
 
         grouped = keep.tile([P, QUERIES + SLOTS, PACK], BF16, align_bytes=64, name="grouped")
         q_grouped, keys = grouped[:, :QUERIES, :], grouped[:, QUERIES:, :]
-        early_parts = [slice(EARLY_CUT, SLOTS), slice(VECTOR_SLOTS, EARLY_CUT)]
-        early = [keep.tile([P, 2, s.stop - s.start], BF16, name=f"early{s.start}") for s in early_parts]
+        early = keep.tile([P, 2, SLOTS - VECTOR_SLOTS], BF16, name="early")
         late = [staged[:, :, :row_words].bitcast(BF16)]
         late.extend(keep.tile([P, 2, s.stop - s.start], BF16, name=f"late{s.start}")[:] for s in scalar_parts[1:])
         first_codes = keep.tile([P, QUERIES + CHUNK], U32, align_bytes=64, name="first_codes")
@@ -79,14 +77,12 @@ def tile_attend_sddmm_kernel(tc, qT, kT, offs, out):
         for j in range(PACK):
             nc.vector.tensor_copy(keys[:, :VECTOR_SLOTS, j], listed(planes[j], 0, VECTOR_SLOTS))
             if j < 2:
-                nc.scalar.activation(early[0][:, j, :], listed(planes[j], EARLY_CUT, SLOTS), COPY)
-                nc.vector.tensor_copy(early[1][:, j, :], listed(planes[j], VECTOR_SLOTS, EARLY_CUT))
+                nc.scalar.activation(early[:, j, :], listed(planes[j], VECTOR_SLOTS, SLOTS), COPY)
             else:
                 for slots, tile in zip(scalar_parts, late):
                     nc.scalar.activation(tile[:, j - 2, :], listed(planes[j], slots.start, slots.stop), COPY)
             if j == 1:
-                for slots, tile in zip(early_parts, early):
-                    nc.vector.tensor_copy(keys[:, slots, 0:2], tile[:].rearrange("p j n -> p n j"))
+                nc.vector.tensor_copy(keys[:, VECTOR_SLOTS:, 0:2], early[:].rearrange("p j n -> p n j"))
 
         for slots, tile in zip(scalar_parts[1:], late[1:]):
             nc.scalar.activation(keys[:, slots, 2:4], tile.rearrange("p j n -> p n j"), COPY)
@@ -120,8 +116,8 @@ def tile_attend_sddmm_kernel(tc, qT, kT, offs, out):
             if c < 2:
                 nc.scalar.copy(result[:, slots], bank[:])
         nc.scalar.activation(listed(windows[0], 0, CHUNK), result[:, :CHUNK], COPY)
-        for bank, slots in zip(banks[2:], chunks[2:]):
-            nc.vector.tensor_copy(result[:, slots], bank[:])
+        nc.vector.tensor_copy(result[:, chunks[2]], banks[2][:])
+        nc.scalar.copy(result[:, chunks[3]], banks[3][:])
         nc.vector.tensor_copy(listed(windows[1], CHUNK, SCATTER_CUT), result[:, CHUNK:SCATTER_CUT])
         nc.scalar.activation(listed(windows[0], SCATTER_CUT, SLOTS), result[:, SCATTER_CUT:], COPY)
         total = keep.tile([P, TOKENS], F32, name="total")

@@ -113,10 +113,9 @@ def tile_attend_sddmm_kernel(tc, qT, kT, offs, out):
                 start=True,
                 stop=True,
             )
-            if c < 2:
+            if c < 3:
                 nc.scalar.copy(result[:, slots], bank[:])
         nc.scalar.activation(listed(windows[0], 0, CHUNK), result[:, :CHUNK], COPY)
-        nc.vector.tensor_copy(result[:, chunks[2]], banks[2][:])
         nc.scalar.copy(result[:, chunks[3]], banks[3][:])
         nc.vector.tensor_copy(listed(windows[1], CHUNK, SCATTER_CUT), result[:, CHUNK:SCATTER_CUT])
         nc.scalar.activation(listed(windows[0], SCATTER_CUT, SLOTS), result[:, SCATTER_CUT:], COPY)

@@ -23,6 +23,7 @@ VECTOR_LAYS = 160
 NEIGHBOURS = 4
 SCATTER_CUT = 384
 STORE_PIECES = 2
+DMA_ALIGN = 256
 
 
 def tile_attend_sddmm_kernel(tc, qT, kT, offs, out):
@@ -39,10 +40,10 @@ def tile_attend_sddmm_kernel(tc, qT, kT, offs, out):
         psum = ctx.enter_context(tc.psum_pool(name="psum", bufs=1))
 
         offsets = keep.tile([P, SLOTS // OFFSETS_A_COLUMN], U16, name="offsets")
-        planes = [keep.tile([P, TOKENS], F32, name=f"plane{j}") for j in range(PACK)]
+        planes = [keep.tile([P, TOKENS], F32, align_bytes=DMA_ALIGN, name=f"plane{j}") for j in range(PACK)]
         row_words = VECTOR_LAYS // 2
-        staged = reuse.tile([P, 2, row_words + PACK * QUERIES], F32, align_bytes=64, offset=0, name="staged")
-        q_raw = staged[:, 0, row_words:]
+        staged = reuse.tile([P, 2, CHUNK + PACK * QUERIES], F32, align_bytes=DMA_ALIGN, offset=0, name="staged")
+        q_raw = staged[:, 0, CHUNK:]
 
         nc.sync.dma_start(planes[0][:], k_rows[0])
         nc.sync.dma_start(offsets[:], offs)
@@ -119,7 +120,7 @@ def tile_attend_sddmm_kernel(tc, qT, kT, offs, out):
         nc.scalar.copy(result[:, chunks[3]], banks[3][:])
         nc.vector.tensor_copy(listed(windows[1], CHUNK, SCATTER_CUT), result[:, CHUNK:SCATTER_CUT])
         nc.scalar.activation(listed(windows[0], SCATTER_CUT, SLOTS), result[:, SCATTER_CUT:], COPY)
-        total = keep.tile([P, TOKENS], F32, name="total")
+        total = keep.tile([P, TOKENS], F32, align_bytes=DMA_ALIGN, name="total")
         width = TOKENS // STORE_PIECES
         for first in range(0, TOKENS, width):
             piece = slice(first, first + width)

from contextlib import ExitStack

import concourse.mybir as mybir

SLOTS, TOKENS, FEATURES, QUERIES = 512, 1024, 512, 128
P = 128
PACK = 4
CHUNK = 128
OFFSETS_A_COLUMN = 16

FLOPS = 2 * QUERIES * FEATURES * SLOTS

F32 = mybir.dt.float32
BF16 = mybir.dt.bfloat16
U32 = mybir.dt.uint32
U16 = mybir.dt.uint16
U8 = mybir.dt.uint8
FP8X4 = mybir.dt.float8_e4m3fn_x4
COPY = mybir.ActivationFunctionType.Copy

VECTOR_SLOTS = 160
VECTOR_LAYS = 160
NEIGHBOURS = 4
SCATTER_CUT = 384
STORE_PIECES = 2
DMA_ALIGN = 256


def tile_attend_sddmm_kernel(tc, qT, kT, offs, out):
    nc = tc.nc
    k_rows = kT.rearrange("(p j) t -> j p t", j=PACK)
    q_rows = qT[0].rearrange("(p j) q -> p (j q)", j=PACK)
    chunks = [slice(c * CHUNK, (c + 1) * CHUNK) for c in range(SLOTS // CHUNK)]
    laid = slice(VECTOR_SLOTS, VECTOR_SLOTS + VECTOR_LAYS)
    scalar_parts = [laid, slice(laid.stop, chunks[2].stop), chunks[3]]

    with ExitStack() as ctx:
        keep = ctx.enter_context(tc.tile_pool(name="keep", bufs=1))
        reuse = ctx.enter_context(tc.tile_pool(name="reuse", bufs=1))
        psum = ctx.enter_context(tc.psum_pool(name="psum", bufs=1))

        offsets = keep.tile([P, SLOTS // OFFSETS_A_COLUMN], U16, name="offsets")
        planes = [keep.tile([P, TOKENS], F32, align_bytes=DMA_ALIGN, name=f"plane{j}") for j in range(PACK)]
        row_words = VECTOR_LAYS // 2
        staged = reuse.tile([P, 2, CHUNK + PACK * QUERIES], F32, align_bytes=DMA_ALIGN, offset=0, name="staged")
        q_raw = staged[:, 0, CHUNK:]

        nc.sync.dma_start(planes[0][:], k_rows[0])
        nc.sync.dma_start(offsets[:], offs)
        for j in range(1, PACK):
            nc.sync.dma_start(planes[j][:], k_rows[j])
        nc.sync.dma_start(q_raw, q_rows)

        warm_in = keep.tile([P, 1], F32, name="warm_in")
        warm_out = keep.tile([P, 1], F32, name="warm_out")
        nc.gpsimd.memset(warm_in[:], 0.0)
        nc.scalar.activation(warm_out[:], warm_in[:], COPY)

        windows = [keep.tile([P, TOKENS], F32, name=f"window{w}") for w in range(2)]
        for window in windows:
            nc.vector.memset(window[:], 0.0)

        grouped = keep.tile([P, QUERIES + SLOTS, PACK], BF16, align_bytes=64, name="grouped")
        q_grouped, keys = grouped[:, :QUERIES, :], grouped[:, QUERIES:, :]
        early = keep.tile([P, 2, SLOTS - VECTOR_SLOTS], BF16, name="early")
        late = [staged[:, :, :row_words].bitcast(BF16)]
        late.extend(keep.tile([P, 2, s.stop - s.start], BF16, name=f"late{s.start}")[:] for s in scalar_parts[1:])
        first_codes = keep.tile([P, QUERIES + CHUNK], U32, align_bytes=64, name="first_codes")
        first_scales = keep.tile([P, QUERIES + CHUNK], U8, align_bytes=64, name="first_scales")
        q_codes, q_scales = first_codes[:, :QUERIES], first_scales[:, :QUERIES]

        def listed(tile, first, end):
            return tile[:].indirect(offsets[:, first // OFFSETS_A_COLUMN : end // OFFSETS_A_COLUMN])

        def quantise(codes, scales, grouped):
            nc.vector.quantize_mx(out=codes.bitcast(FP8X4), scales=scales, in_=grouped.rearrange("p n j -> p (n j)"))

        for j in range(PACK):
            nc.vector.tensor_copy(keys[:, :VECTOR_SLOTS, j], listed(planes[j], 0, VECTOR_SLOTS))
            if j < 2:
                nc.scalar.activation(early[:, j, :], listed(planes[j], VECTOR_SLOTS, SLOTS), COPY)
            else:
                for slots, tile in zip(scalar_parts, late):
                    nc.scalar.activation(tile[:, j - 2, :], listed(planes[j], slots.start, slots.stop), COPY)
            if j == 1:
                nc.vector.tensor_copy(keys[:, VECTOR_SLOTS:, 0:2], early[:].rearrange("p j n -> p n j"))

        for slots, tile in zip(scalar_parts[1:], late[1:]):
            nc.scalar.activation(keys[:, slots, 2:4], tile.rearrange("p j n -> p n j"), COPY)

        nc.vector.tensor_copy(
            q_grouped.rearrange("p (c i) j -> p c j i", i=NEIGHBOURS),
            q_raw.rearrange("p (j c i) -> p c j i", j=PACK, i=NEIGHBOURS),
        )
        nc.vector.tensor_copy(keys[:, laid, 2:4], late[0].rearrange("p j n -> p n j"))
        quantise(first_codes[:], first_scales[:], grouped[:, : QUERIES + CHUNK, :])

        result = keep.tile([QUERIES, SLOTS], F32, name="result")
        banks = [psum.tile([QUERIES, CHUNK], F32, name=f"acc{c}") for c in range(len(chunks))]
        for c, slots in enumerate(chunks):
            if c == 0:
                codes, scales = first_codes[:, QUERIES:], first_scales[:, QUERIES:]
            else:
                codes = reuse.tile([P, CHUNK], U32, align_bytes=64, offset=4 * CHUNK * c, name=f"codes{c}")[:]
                scales = keep.tile([P, CHUNK], U8, align_bytes=64, name=f"scales{c}")[:]
                quantise(codes, scales, keys[:, slots, :])
            bank = banks[c]
            nc.tensor.matmul_mx(
                out=bank[:],
                lhsT=q_codes.bitcast(FP8X4),
                lhsT_scale=q_scales,
                rhs=codes.bitcast(FP8X4),
                rhs_scale=scales,
                start=True,
                stop=True,
            )
            if c < 3:
                nc.scalar.copy(result[:, slots], bank[:])
        nc.scalar.activation(listed(windows[0], 0, CHUNK), result[:, :CHUNK], COPY)
        nc.scalar.copy(result[:, chunks[3]], banks[3][:])
        nc.vector.tensor_copy(listed(windows[1], CHUNK, SCATTER_CUT), result[:, CHUNK:SCATTER_CUT])
        nc.scalar.activation(listed(windows[0], SCATTER_CUT, SLOTS), result[:, SCATTER_CUT:], COPY)
        total = keep.tile([P, TOKENS], F32, align_bytes=DMA_ALIGN, name="total")
        width = TOKENS // STORE_PIECES
        for first in range(0, TOKENS, width):
            piece = slice(first, first + width)
            nc.vector.tensor_add(total[:, piece], windows[0][:, piece], windows[1][:, piece])
            nc.sync.dma_start(out[0][:, piece], total[:, piece])
